import numpy as np, ml_dtypes
CORES = [30,158,46,174,86,214]
N = 6
import mx_ref
NC, G = 256, 4
C = np.float32(0.047)
BF = ml_dtypes.bfloat16
def cut(t, i, w=512):
    return t[:, w * i:w * i + w]
def tile(rs):
    return np.stack(rs, axis=2).reshape(128, -1).astype(BF)
def layer(w, X):
    out = []
    for i in range(G):
        for t in range(len(X)):
            p = mx_ref.matmul(mx_ref.quantize(cut(w, len(X) * i + t)), X[t])
            z = p if t == 0 else z + p
        out.append(z)
    return out
def setup_inputs(rng):
    def f(*shape):
        return mx_ref.flush((rng.standard_normal(shape, dtype=np.float32) * np.exp2(rng.integers(-2, 3, shape[:-1] + (1,)))).astype(BF))
    return {"x": f(N, 128, 4 * NC), "w": f(N, 128, 512), "a": f(N, 128, 4 * 512), "bb": f(N, 128, 512)}
def setup_inputs_blocks(rng):
    d = setup_inputs(rng)
    for k in ("x", "w", "bb", "a"): d[k] = mx_ref.spread(d[k], rng, 4)
    return d
def setup_inputs_wide(rng):
    d = setup_inputs(rng)
    for k in ("x", "w", "bb", "a"): d[k] = mx_ref.flush((d[k].astype(np.float32) * np.exp2(rng.integers(-6, 7, (N, 1, 1))).astype(np.float32)).astype(BF))
    return d
def setup_inputs_zeros(rng):
    d = setup_inputs(rng); v = d["x"].reshape(N, 128, -1, 4).copy()
    v[np.broadcast_to((rng.random((N, 1, v.shape[2], 1)) < 0.33), v.shape)] = 0
    d["x"] = v.reshape(d["x"].shape)
    return d
def reference(x, w, a, bb):
    X = [mx_ref.quantize(x[j]) for j in range(N)]
    T = [mx_ref.quantize(tile([z * C for z in layer(a[j], [X[j]])])) for j in range(N)]
    y = np.zeros((N, 128, N * NC), np.float32)
    for r in range(N):
        qw = mx_ref.quantize(w[r]); qb = mx_ref.quantize(bb[r])
        for j in range(N):
            y[r][:, NC * j:NC * j + NC] = mx_ref.matmul(qw, X[j]) + mx_ref.matmul(qb, T[j])
    return {"y": y}

from concourse.bass import DstId, RemoteDMATransfer
from concourse.mybir import dt, AluOpType, ActivationFunctionType

N, NC, G = 6, 256, 4
MACHINE = 256
C = 0.047
X_HELPED = (1, 2, 3)
T_HELPED = (4, 5)

SCRATCH = {
    "xb": ("sbuf", [128, 4 * NC], "bfloat16"),
    "ab": ("sbuf", [128, G * 512], "bfloat16"),
    "wb": ("sbuf", [128, 512], "bfloat16"),
    "bbb": ("sbuf", [128, 512], "bfloat16"),
    "tb": ("sbuf", [128, 4 * NC], "bfloat16"),
    "xc": ("sbuf", [128, N * NC], "float8_e4m3fn_x4"),
    "tc": ("sbuf", [128, N * NC], "float8_e4m3fn_x4"),
    "pl": ("sbuf", [128, N * 2 * NC], "uint8"),
    "ac": ("sbuf", [128, G * 128], "float8_e4m3fn_x4"),
    "ap": ("sbuf", [128, G * 128], "uint8"),
    "wc": ("sbuf", [128, 128], "float8_e4m3fn_x4"),
    "wp": ("sbuf", [128, 128], "uint8"),
    "bc": ("sbuf", [128, 128], "float8_e4m3fn_x4"),
    "bp": ("sbuf", [128, 128], "uint8"),
    "yb": ("sbuf", [128, N * NC], "float32"),
    "ps": ("psum", [128, 512 * 8], "float32"),
}
SEMAPHORES = (["lx", "la0", "la1", "lb", "lw", "qx", "qt", "qb", "qw", "sent"]
              + [p + str(i) for p in ("qa", "z", "e") for i in range(G)]
              + [p + str(j) for p in ("X", "P", "T", "mm", "ev", "st") for j in range(N)])


def rank_program(g, core, T, topo):
    S = T.sem
    cores = list(T.cores)

    def same_chip(a, b):
        return topo.host(a) == topo.host(b) and topo.chip(a) == topo.chip(b)

    def helpers(rc):
        return [c for c in range(MACHINE) if same_chip(c, rc) and topo.die(c) != topo.die(rc)
                and all(topo.may_write(c, d) for d in cores if d != rc)]

    def bits(m):
        return bin(m).count("1")

    def piece(kind, j):
        if kind == "X":
            return T.xc[:, NC * j:NC * j + NC].bitcast(dt.uint8)
        if kind == "T":
            return T.tc[:, NC * j:NC * j + NC].bitcast(dt.uint8)
        return T.pl[:, 2 * NC * j:2 * NC * j + 2 * NC]

    def far_mask(src, dests):
        m = topo.mask(src, dests[0])
        for d in dests[1:]:
            m &= topo.mask(src, d)
        return m

    def transfer(kind, j, dests, mask):
        ids = []
        for d in dests:
            rid, pid = topo.addr(d, core)
            ids.append(DstId(rid=rid, pnc=pid))
        return RemoteDMATransfer(dst_ids=ids, dma_engine_mask=mask, remote_sem=S[kind + str(j)],
                                 srcs=[piece(kind, j)], dsts=[piece(kind, j) for _ in dests])

    def dests_of(j, offsets):
        return [cores[(j + o) % N] for o in offsets]

    rank = T.rank_of(core)
    if rank is None:
        for j, rc in enumerate(cores):
            if not same_chip(core, rc):
                continue
            hs = helpers(rc)
            if core == hs[0]:
                kinds, offs = ("X",), X_HELPED
            elif core == hs[1]:
                kinds, offs = ("P", "T"), T_HELPED
            else:
                continue
            far = dests_of(j, offs)
            mask = far_mask(core, far)
            near = topo.mask(rc, core) & ~far_mask(rc, dests_of(j, range(1, N)))
            for k in kinds:
                g.wait_ge(S[k + str(j)], bits(near))
                g.remote_dma_fused([transfer(k, j, far, mask)], local_sem=S.sent)
            g.wait_ge(S.sent, bits(mask) * len(kinds))
        return

    r = rank
    hx, ht = helpers(core)[:2]

    g.sync.dma_start(T.xb[:], T.x[:]).then_inc(S.lx, 16)
    g.scalar.dma_start(T.ab[:, 0:1024], T.a[:, 0:1024]).then_inc(S.la0, 16)
    g.sync.dma_start(T.ab[:, 1024:2048], T.a[:, 1024:2048]).then_inc(S.la1, 16)
    g.sync.dma_start(T.bbb[:], T.bb[:]).then_inc(S.lb, 16)
    g.sync.dma_start(T.wb[:], T.w[:]).then_inc(S.lw, 16)

    xs = (T.xc[:, NC * r:NC * r + NC], T.pl[:, 2 * NC * r:2 * NC * r + NC])
    ts = (T.tc[:, NC * r:NC * r + NC], T.pl[:, 2 * NC * r + NC:2 * NC * r + 2 * NC])

    def a_of(i):
        return T.ac[:, 128 * i:128 * i + 128], T.ap[:, 128 * i:128 * i + 128]

    def bank(b):
        return T.ps[:, 512 * b:512 * b + NC]

    v = g.vector
    v.wait_ge(S.lx, 16)
    v.quantize_mx(xs[0], xs[1], T.xb[:]).then_inc(S.qx, 1)
    for i in range(G):
        if i % 2 == 0:
            v.wait_ge(S["la%d" % (i // 2)], 16)
        ac, ap = a_of(i)
        v.quantize_mx(ac, ap, T.ab[:, 512 * i:512 * i + 512]).then_inc(S["qa%d" % i], 1)
    for i in range(G):
        q = g.scalar if i % 2 == 0 else v
        q.wait_ge(S["z%d" % i], 1)
        out = T.tb[:, i:4 * NC:4]
        if i % 2 == 0:
            q.activation(out, bank(i), ActivationFunctionType.Copy, scale=C).then_inc(S["e%d" % i], 1)
        else:
            q.tensor_scalar(out, bank(i), C, None, AluOpType.mult).then_inc(S["e%d" % i], 1)
    for i in range(G):
        v.wait_ge(S["e%d" % i], 1)
    v.quantize_mx(ts[0], ts[1], T.tb[:]).then_inc(S.qt, 1)
    v.wait_ge(S.lw, 16)
    v.quantize_mx(T.wc[:], T.wp[:], T.wb[:]).then_inc(S.qw, 1)
    v.wait_ge(S.lb, 16)
    v.quantize_mx(T.bc[:], T.bp[:], T.bbb[:]).then_inc(S.qb, 1)

    lo = far_mask(core, dests_of(r, range(1, N)))
    total = 0
    for kind, helper, helped, ready in (("X", hx, X_HELPED, "qx"), ("P", ht, T_HELPED, "qt"), ("T", ht, T_HELPED, None)):
        if ready:
            g.wait_ge(S[ready], 1)
        hi = topo.mask(core, helper) & ~lo
        direct = dests_of(r, [o for o in range(1, N) if o not in helped])
        g.remote_dma_fused([transfer(kind, r, [helper], hi), transfer(kind, r, direct, lo)], local_sem=S.sent)
        total += bits(hi) + bits(lo)

    t = g.tensor
    t.wait_ge(S.qx, 1)
    for i in range(G):
        t.wait_ge(S["qa%d" % i], 1)
        ac, ap = a_of(i)
        t.matmul_mx(bank(i), ac, ap, xs[0], xs[1], True, True).then_inc(S["z%d" % i], 1)
    direct = [o for o in range(1, N) if o not in T_HELPED]
    order = [(0,), tuple(direct), tuple(T_HELPED)]
    flat = [o for grp in order for o in grp]
    where = {o: (4, 5, 6, 7, 0, 1)[n] for n, o in enumerate(flat)}
    src = {o: (r - o) % N for o in flat}
    t.wait_ge(S.qw, 1)
    for grp in order:
        for o in grp:
            j = src[o]
            if o:
                t.wait_ge(S["P%d" % j], bits(lo))
                t.wait_ge(S["X%d" % j], bits(lo))
            else:
                t.wait_ge(S.qt, 1)
            if where[o] < G:
                t.wait_ge(S["e%d" % where[o]], 1)
            t.matmul_mx(bank(where[o]), T.wc[:], T.wp[:], T.xc[:, NC * j:NC * j + NC],
                        T.pl[:, 2 * NC * j:2 * NC * j + NC], True, False)
        for o in grp:
            j = src[o]
            if o:
                t.wait_ge(S["T%d" % j], bits(lo))
            else:
                t.wait_ge(S.qb, 1)
            t.matmul_mx(bank(where[o]), T.bc[:], T.bp[:], T.tc[:, NC * j:NC * j + NC],
                        T.pl[:, 2 * NC * j + NC:2 * NC * j + 2 * NC], False, True).then_inc(S["mm%d" % j], 1)

    for n, o in enumerate(flat):
        j = src[o]
        blk = T.yb[:, NC * j:NC * j + NC]
        if n % 2 == 0:
            g.scalar.wait_ge(S["mm%d" % j], 1)
            g.scalar.activation(blk, bank(where[o]), ActivationFunctionType.Copy).then_inc(S["ev%d" % j], 1)
            q = g.scalar
        else:
            v.wait_ge(S["mm%d" % j], 1)
            v.tensor_copy(blk, bank(where[o])).then_inc(S["ev%d" % j], 1)
            q = g.sync
        q.wait_ge(S["ev%d" % j], 1)
        q.dma_start(T.y[:, NC * j:NC * j + NC], blk).then_inc(S["st%d" % j], 16)
    for n, o in enumerate(flat):
        q = g.scalar if n % 2 == 0 else g.sync
        q.wait_ge(S["st%d" % src[o]], 16)
    g.wait_ge(S.sent, total)
